import numpy as np
import ml_dtypes


def mxq(x, axis, fmt="e4m3"):
    dtype, down = {"e4m3": (ml_dtypes.float8_e4m3fn, 7), "e5m2": (ml_dtypes.float8_e5m2, 14)}[fmt]
    v = np.moveaxis(np.asarray(x, np.float32).astype(ml_dtypes.bfloat16).astype(np.float64), axis, -1)
    blocks = v.reshape(v.shape[:-1] + (-1, 32))
    amax = np.abs(blocks).max(-1, keepdims=True)
    byte = np.maximum(np.where(amax > 0, np.frexp(amax)[1] - 1 + 127, 0) - down, 1)
    scale = np.exp2(byte - 127.0)
    codes = (blocks / scale).astype(np.float32).astype(dtype).astype(np.float64)
    return np.moveaxis((codes * scale).reshape(v.shape), -1, axis)


WIDE = False


def mx_kscale(k):
    if not WIDE:
        return np.ones(k)
    levels = np.array([30, -30])
    if k % 512:
        return np.exp2(np.random.permutation(np.resize(levels, k // 32))).repeat(32)
    a = np.empty((k // 512, 16))
    for p in range(k // 512):
        a[p, :8] = np.random.permutation(np.resize(levels, 8))
        for g in range(8):
            far = levels[np.abs(levels - a[p, g]) >= 10]
            a[p, g + 8] = far[np.random.randint(len(far))]
    return np.exp2(a.ravel()).repeat(32)


BF16 = ml_dtypes.bfloat16


def bf(x):
    return np.asarray(x, np.float32).astype(BF16)


def f64(x):
    return np.asarray(x).astype(np.float64)


E, KI, KH, R = 1024, 2048, 1024, 1024


def setup_inputs():
    s = mx_kscale(KI)
    u = mx_kscale(KH)
    tail = np.exp(0.7 * np.random.standard_normal((KH, R)))
    return {"psi": bf(np.random.standard_normal((E, R))),
            "chi_in": bf(2.0 * np.random.standard_normal((KI, R)) / s[:, None]),
            "chi_halo": bf(np.random.standard_normal((KH, R)) * tail * u[:, None]),
            "hop_in": bf(2.0 * np.random.standard_normal((E, KI)) / np.sqrt(KI) * s),
            "hop_halo": bf(2.0 * np.random.standard_normal((KH, E)) / np.sqrt(KH) / u[:, None]),
            "kappa": bf(0.4 * (1.0 + 0.1 * np.random.standard_normal(R)))}


def reference(psi, chi_in, chi_halo, hop_in, hop_halo, kappa):
    a = mxq(f64(hop_in), 1, "e4m3")
    b = mxq(f64(chi_in), 0, "e4m3")
    c = mxq(f64(hop_halo), 0, "e4m3")
    d = mxq(f64(chi_halo), 0, "e5m2")
    hop = (a @ b) + (c.T @ d)
    return f64(psi) - np.square(f64(kappa))[None, :] * hop

@@ -1,0 +1,271 @@
+from contextlib import ExitStack
+
+import concourse.mybir as mybir
+from concourse.masks import make_identity
+
+E, KI, KH, R = 1024, 2048, 1024, 1024
+FLOPS = 2 * E * R * (KI + KH) + 3 * E * R
+
+F32 = mybir.dt.float32
+BF16 = mybir.dt.bfloat16
+U32 = mybir.dt.uint32
+U8 = mybir.dt.uint8
+E4M3 = mybir.dt.float8_e4m3fn_x4
+E5M2 = mybir.dt.float8_e5m2_x4
+ALU = mybir.AluOpType
+
+P = 128
+PACK = 4
+K_PASS = P * PACK
+INNER = KI // K_PASS
+HALO = KH // K_PASS
+PASSES = INNER + HALO
+BLOCKS = E // P
+HALF = R // 2
+
+V_EARLY = 288
+V_LATE = 160
+OPEN = 6
+LAG = 1
+ORDER = "h0 c0 h1 h2 c1 h3 c2 c3 h4 l0 c4 h5 l1 c5 h6 h7"
+LATE = "x0 c0 c1 q0 c2 c3 x1 c4 c5 q1 c6 x2 c7 q2 x3 f0 q3 x4 f1 q4 x5 f2 q5 f3 f4 f5 f6 f7"
+GROUPED = 8
+GPSIMD_ADDS = tuple((b, 0) for b in range(8))
+
+
+def tile_wilson_schur_hop_s2_kernel(tc, psi, chi_in, chi_halo, hop_in, hop_halo, kappa, out):
+    nc = tc.nc
+
+    with ExitStack() as ctx:
+        const = ctx.enter_context(tc.tile_pool(name="const", bufs=1))
+        raw = ctx.enter_context(tc.tile_pool(name="raw", bufs=8))
+        keep = ctx.enter_context(tc.tile_pool(name="keep", bufs=1))
+        stage = ctx.enter_context(tc.tile_pool(name="stage", bufs=3))
+        late = ctx.enter_context(tc.tile_pool(name="late", bufs=8))
+        psum = ctx.enter_context(tc.psum_pool(name="psum", bufs=1))
+        ctx.enter_context(tc.manual_schedule())
+
+        hop_raw, chi_raw, halo_raw, psi_raw = {}, {}, {}, {}
+        codes, planes = {}, {}
+        grouped = {}
+        turned = {}
+        acc = {}
+        product = {}
+
+        def load(chunk):
+            kind, i = chunk[0], chunk[1]
+            if kind == "hop":
+                tile = raw.tile([P, KI], BF16, name="hop_raw", bufs=8, align_bytes=64)
+                rows = slice(i * P, (i + 1) * P)
+                if i == 0:
+                    for lo in (0, KI // 2):
+                        nc.sync.dma_start(out=tile[:, lo : lo + KI // 2], in_=hop_in[rows, lo : lo + KI // 2])
+                else:
+                    nc.sync.dma_start(out=tile[:], in_=hop_in[rows, :])
+                hop_raw[i] = tile
+            elif kind == "chi":
+                half = chunk[2]
+                tile = raw.tile([P, PACK, HALF], BF16, name="chi_raw", bufs=8, align_bytes=64)
+                src = chi_in if i < INNER else chi_halo
+                k0 = (i if i < INNER else i - INNER) * K_PASS
+                rows = src[k0 : k0 + K_PASS, half * HALF : (half + 1) * HALF]
+                nc.sync.dma_start(out=tile[:], in_=rows.rearrange("(p j) r -> p j r", j=PACK))
+                chi_raw[i, half] = tile
+            elif kind == "halo":
+                tile = raw.tile([P, PACK, E], BF16, name="halo_raw", bufs=2, align_bytes=64)
+                rows = hop_halo[i * K_PASS : (i + 1) * K_PASS, :]
+                nc.sync.dma_start(out=tile[:], in_=rows.rearrange("(p j) e -> p j e", j=PACK))
+                halo_raw[i] = tile
+            else:
+                tile = raw.tile([P, BLOCKS // 2, HALF], BF16, name="psi_raw", bufs=4, align_bytes=64)
+                half = chunk[2]
+                rows = psi[i * (E // 2) : (i + 1) * (E // 2), half * HALF : (half + 1) * HALF]
+                nc.sync.dma_start(out=tile[:], in_=rows.rearrange("(b p) r -> p b r", p=P))
+                psi_raw[i, half] = tile
+
+        def turn(b):
+            words = hop_raw[b][:].bitcast(F32)
+            for h in range(2):
+                bank = psum.tile([P, 4, P], F32, name="turn_bank", tag="turn", bufs=2)
+                for s in range(4):
+                    g, u = 2 * h + s // 2, s % 2
+                    w0 = g * (K_PASS // 2)
+                    nc.tensor.transpose(bank[:, s, :], words[:, w0 + u : w0 + K_PASS // 2 : 2], identity[:])
+                turned[b, h] = bank
+
+        def interleave(engine_copy, dst, src, lo, hi):
+            engine_copy(
+                out=dst[:, lo:hi, :].rearrange("p (c i) t -> p c t i", i=4),
+                in_=src[:, :, lo:hi].rearrange("p t (c i) -> p c t i", i=4),
+            )
+
+        def spread(unit):
+            kind, i = unit[0], unit[1]
+            tile = stage.tile([P, 4, P, PACK], BF16, name="grouped", bufs=GROUPED, align_bytes=64)
+            if kind == "hop":
+                for h in range(2):
+                    dst = tile[:, 2 * h : 2 * h + 2, :, :].rearrange("p g r t -> p g (r t)").bitcast(F32)
+                    nc.scalar.copy(
+                        out=dst.rearrange("p g (r u) -> p g r u", u=2),
+                        in_=turned[i, h][:].rearrange("p (g u) r -> p g r u", u=2),
+                    )
+            else:
+                n = unit[2]
+                cut = V_EARLY if kind == "halo" or n == 0 else V_LATE
+                rows = chi_raw[i, n] if kind == "chi" else halo_raw[i][:, :, n * HALF : (n + 1) * HALF]
+                flat = tile[:].rearrange("p g r t -> p (g r) t")
+                interleave(nc.scalar.copy, flat, rows, cut, HALF)
+                interleave(nc.vector.tensor_copy, flat, rows, 0, cut)
+            grouped[unit] = tile
+
+        def quantize(unit):
+            fmt = E5M2 if unit[0] == "chi" and unit[1] >= INNER else E4M3
+            name = "_".join(str(x) for x in unit)
+            code = keep.tile([P, HALF], U32, name="codes_" + name, align_bytes=64)
+            plane = keep.tile([P, HALF], U8, name="plane_" + name, align_bytes=64)
+            nc.vector.quantize_mx(
+                out=code[:].bitcast(fmt), scales=plane[:], in_=grouped[unit][:].rearrange("p g r t -> p (g r t)")
+            )
+            codes[unit], planes[unit] = code, plane
+
+        def multiply(b, half, p, start, stop):
+            if p < INNER:
+                w, cols = ("hop", b), slice(p * P, (p + 1) * P)
+            else:
+                w, cols = ("halo", p - INNER, b // 4), slice(b % 4 * P, (b % 4 + 1) * P)
+            x = ("chi", p, half)
+            if start:
+                tag = "acc" if b < OPEN else "turn"
+                acc[b, half] = psum.tile([P, HALF], F32, name="acc_bank", tag=tag, bufs=OPEN if b < OPEN else 2)
+            nc.tensor.matmul_mx(
+                out=acc[b, half][:],
+                lhsT=codes[w][:, cols].bitcast(E4M3),
+                lhsT_scale=planes[w][:, cols],
+                rhs=codes[x][:].bitcast(E4M3 if p < INNER else E5M2),
+                rhs_scale=planes[x][:],
+                start=start,
+                stop=stop,
+            )
+
+        def scale(b, half):
+            t = late.tile([P, HALF], F32, name="product", bufs=8)
+            nc.vector.tensor_tensor(
+                out=t[:], in0=acc[b, half][:], in1=minus_k2[:, half * HALF : (half + 1) * HALF], op=ALU.mult
+            )
+            product[b, half] = t
+
+        def finish(b, half):
+            o = late.tile([P, HALF], F32, name="result", bufs=6)
+            engine = nc.gpsimd if (b, half) in GPSIMD_ADDS else nc.vector
+            field = psi_raw[b // 4, half][:, b % 4, :]
+            engine.tensor_tensor(out=o[:], in0=product[b, half][:], in1=field, op=ALU.add)
+            nc.sync.dma_start(out=out[b * P : (b + 1) * P, half * HALF : (half + 1) * HALF], in_=o[:])
+
+        def eval_chunk(x):
+            return {"h": ("hop", int(x[1])), "c": ("chi", int(x[1]), 0), "l": ("halo", int(x[1]))}[x[0]]
+
+        identity = const.tile([P, P], F32, name="identity")
+        make_identity(nc, identity[:])
+        k_rows = const.tile([P, P], BF16, name="k_rows")
+        nc.vector.memset(k_rows[:], 0.0)
+        nc.scalar.dma_start(out=k_rows[0:BLOCKS, :], in_=kappa.rearrange("(m j) -> m j", j=P))
+        k_rows32 = const.tile([P, P], F32, name="k_rows32")
+        k_cols = const.tile([P, BLOCKS], F32, name="k_cols")
+        minus_k2_cols = const.tile([P, BLOCKS], F32, name="minus_k2_cols")
+        minus_k2 = const.tile([P, R], F32, name="minus_k2")
+
+        order = [eval_chunk(x) for x in ORDER.split()]
+        for chunk in order:
+            load(chunk)
+        for chunk in (("chi", 0, 1), ("chi", 1, 1), ("psi", 0, 0), ("psi", 1, 0)):
+            load(chunk)
+
+        def kappa_front():
+            nc.vector.tensor_copy(out=k_rows32[:], in_=k_rows[:])
+            k_bank = psum.tile([P, 4, P], F32, name="k_bank", tag="acc", bufs=OPEN)
+            nc.tensor.transpose(k_bank[:, 0, :], k_rows32[:], identity[:])
+            nc.vector.tensor_copy(out=k_cols[:], in_=k_bank[:, 0, 0:BLOCKS])
+            nc.vector.scalar_tensor_tensor(
+                out=minus_k2_cols[:], in0=k_cols[:], scalar=-1.0, in1=k_cols[:], op0=ALU.mult, op1=ALU.mult
+            )
+
+        k_banks = []
+
+        def kappa_spread():
+            for half in range(2):
+                k_bank = psum.tile([P, 4, P], F32, name="k_bank", tag="acc", bufs=OPEN)
+                for s in range(4):
+                    m = half * 4 + s
+                    nc.tensor.transpose(k_bank[:, s, :], minus_k2_cols[:, m : m + 1].to_broadcast([P, P]), identity[:])
+                k_banks.append(k_bank)
+
+        def kappa_back():
+            for half in range(2):
+                nc.scalar.copy(
+                    out=minus_k2[:, half * HALF : (half + 1) * HALF], in_=k_banks[half][:].rearrange("p s n -> p (s n)")
+                )
+
+        units = []
+        for chunk in order:
+            units += [("halo", chunk[1], 0), ("halo", chunk[1], 1)] if chunk[0] == "halo" else [chunk]
+        have_hop, have_halo, have_chi, counts = [], [], [], {}
+
+        def newly_enabled(unit):
+            kind, i = unit[0], unit[1]
+            if kind == "hop":
+                if i >= OPEN:
+                    return []
+                have_hop.append(i)
+                return [(i, p) for p in have_chi if p < INNER or (p - INNER, i // 4) in have_halo]
+            if kind == "chi":
+                have_chi.append(i)
+                return [(b, i) for b in have_hop if i < INNER or (i - INNER, b // 4) in have_halo]
+            have_halo.append((i, unit[2]))
+            return [(b, INNER + i) for b in have_hop if INNER + i in have_chi and b // 4 == unit[2]]
+
+        turn(units[0][1])
+        kappa_front()
+        kappa_spread()
+        for i in range(len(units) + LAG + 1):
+            if i < len(units):
+                spread(units[i])
+            if i + 1 < len(units) and units[i + 1][0] == "hop":
+                turn(units[i + 1][1])
+            if i == 6:
+                kappa_back()
+            if 0 <= i - LAG < len(units):
+                quantize(units[i - LAG])
+            if i - LAG - 1 >= 0:
+                for b, p in newly_enabled(units[i - LAG - 1]):
+                    counts[b] = counts.get(b, 0) + 1
+                    multiply(b, 0, p, counts[b] == 1, counts[b] == PASSES)
+
+        for b in range(OPEN, BLOCKS):
+            for p in range(PASSES):
+                multiply(b, 0, p, p == 0, p == PASSES - 1)
+
+        for p in range(2, PASSES):
+            load(("chi", p, 1))
+        load(("psi", 0, 1))
+        load(("psi", 1, 1))
+        for step in LATE.split():
+            j = int(step[1:])
+            if step.startswith("x"):
+                spread(("chi", j, 1))
+            elif step.startswith("q"):
+                quantize(("chi", j, 1))
+            elif step.startswith("c"):
+                scale(j, 0)
+            else:
+                finish(j, 0)
+
+        for p in range(2):
+            for b in range(BLOCKS):
+                multiply(b, 1, p, p == 0, False)
+        for b in range(BLOCKS):
+            for p in range(2, PASSES):
+                multiply(b, 1, p, False, p == PASSES - 1)
+            scale(b, 1)
+            if b >= 1:
+                finish(b - 1, 1)
+        finish(BLOCKS - 1, 1)

@@ -23,14 +23,18 @@ PASSES = INNER + HALO
 BLOCKS = E // P
 HALF = R // 2
 
-V_EARLY = 288
-V_LATE = 160
+V_EARLY = 320
+V_LATE = 64
 OPEN = 6
-LAG = 1
-ORDER = "h0 c0 h1 h2 c1 h3 c2 c3 h4 l0 c4 h5 l1 c5 h6 h7"
-LATE = "x0 c0 c1 q0 c2 c3 x1 c4 c5 q1 c6 x2 c7 q2 x3 f0 q3 x4 f1 q4 x5 f2 q5 f3 f4 f5 f6 f7"
+LAG = 2
+ORDER = "h0 c0 h1 c1 h2 a0 h3 c2 c3 h4 b0 a1 c4 h5 c5 h6 b1 n0 n1 n2 p0 h7 n3 n4 p2 n5 p1 p3"
+DC = 2
+DF = 1
+FIRST = 4
+DF2 = 2
+KAPPA = 1
 GROUPED = 8
-GPSIMD_ADDS = tuple((b, 0) for b in range(8))
+GPSIMD_ADDS = ((0, 1), (1, 1), (2, 1), (4, 1), (6, 1))
 
 
 def tile_wilson_schur_hop_s2_kernel(tc, psi, chi_in, chi_halo, hop_in, hop_halo, kappa, out):
@@ -51,6 +55,7 @@ def tile_wilson_schur_hop_s2_kernel(tc, psi, chi_in, chi_halo, hop_in, hop_halo,
         turned = {}
         acc = {}
         product = {}
+        free_banks, bank_of = list(range(OPEN)), {}
 
         def load(chunk):
             kind, i = chunk[0], chunk[1]
@@ -72,10 +77,11 @@ def tile_wilson_schur_hop_s2_kernel(tc, psi, chi_in, chi_halo, hop_in, hop_halo,
                 nc.sync.dma_start(out=tile[:], in_=rows.rearrange("(p j) r -> p j r", j=PACK))
                 chi_raw[i, half] = tile
             elif kind == "halo":
-                tile = raw.tile([P, PACK, E], BF16, name="halo_raw", bufs=2, align_bytes=64)
-                rows = hop_halo[i * K_PASS : (i + 1) * K_PASS, :]
+                part = chunk[2]
+                tile = raw.tile([P, PACK, HALF], BF16, name="halo_raw", bufs=4, align_bytes=64)
+                rows = hop_halo[i * K_PASS : (i + 1) * K_PASS, part * HALF : (part + 1) * HALF]
                 nc.sync.dma_start(out=tile[:], in_=rows.rearrange("(p j) e -> p j e", j=PACK))
-                halo_raw[i] = tile
+                halo_raw[i, part] = tile
             else:
                 tile = raw.tile([P, BLOCKS // 2, HALF], BF16, name="psi_raw", bufs=4, align_bytes=64)
                 half = chunk[2]
@@ -112,7 +118,7 @@ def tile_wilson_schur_hop_s2_kernel(tc, psi, chi_in, chi_halo, hop_in, hop_halo,
             else:
                 n = unit[2]
                 cut = V_EARLY if kind == "halo" or n == 0 else V_LATE
-                rows = chi_raw[i, n] if kind == "chi" else halo_raw[i][:, :, n * HALF : (n + 1) * HALF]
+                rows = chi_raw[i, n] if kind == "chi" else halo_raw[i, n]
                 flat = tile[:].rearrange("p g r t -> p (g r) t")
                 interleave(nc.scalar.copy, flat, rows, cut, HALF)
                 interleave(nc.vector.tensor_copy, flat, rows, 0, cut)
@@ -135,8 +141,10 @@ def tile_wilson_schur_hop_s2_kernel(tc, psi, chi_in, chi_halo, hop_in, hop_halo,
                 w, cols = ("halo", p - INNER, b // 4), slice(b % 4 * P, (b % 4 + 1) * P)
             x = ("chi", p, half)
             if start:
-                tag = "acc" if b < OPEN else "turn"
-                acc[b, half] = psum.tile([P, HALF], F32, name="acc_bank", tag=tag, bufs=OPEN if b < OPEN else 2)
+                bank = free_banks[0]
+                free_banks.remove(bank)
+                bank_of[b, half] = bank
+                acc[b, half] = psum.tile([P, HALF], F32, name="acc_bank", tag="acc%d" % bank, bufs=1)
             nc.tensor.matmul_mx(
                 out=acc[b, half][:],
                 lhsT=codes[w][:, cols].bitcast(E4M3),
@@ -153,6 +161,7 @@ def tile_wilson_schur_hop_s2_kernel(tc, psi, chi_in, chi_halo, hop_in, hop_halo,
                 out=t[:], in0=acc[b, half][:], in1=minus_k2[:, half * HALF : (half + 1) * HALF], op=ALU.mult
             )
             product[b, half] = t
+            free_banks.append(bank_of[b, half])
 
         def finish(b, half):
             o = late.tile([P, HALF], F32, name="result", bufs=6)
@@ -162,7 +171,8 @@ def tile_wilson_schur_hop_s2_kernel(tc, psi, chi_in, chi_halo, hop_in, hop_halo,
             nc.sync.dma_start(out=out[b * P : (b + 1) * P, half * HALF : (half + 1) * HALF], in_=o[:])
 
         def eval_chunk(x):
-            return {"h": ("hop", int(x[1])), "c": ("chi", int(x[1]), 0), "l": ("halo", int(x[1]))}[x[0]]
+            i = int(x[1])
+            return {"h": ("hop", i), "c": ("chi", i, 0), "n": ("chi", i, 1), "a": ("halo", i, 0), "b": ("halo", i, 1), "p": ("psi", i // 2, i % 2)}[x[0]]
 
         identity = const.tile([P, P], F32, name="identity")
         make_identity(nc, identity[:])
@@ -174,26 +184,38 @@ def tile_wilson_schur_hop_s2_kernel(tc, psi, chi_in, chi_halo, hop_in, hop_halo,
         minus_k2_cols = const.tile([P, BLOCKS], F32, name="minus_k2_cols")
         minus_k2 = const.tile([P, R], F32, name="minus_k2")
 
-        order = [eval_chunk(x) for x in ORDER.split()]
-        for chunk in order:
-            load(chunk)
-        for chunk in (("chi", 0, 1), ("chi", 1, 1), ("psi", 0, 0), ("psi", 1, 0)):
-            load(chunk)
+        loads = [eval_chunk(x) for x in ORDER.split()]
+        units = [u for u in loads if u[0] != "psi"]
+        waiting = list(loads)
 
-        def kappa_front():
+        def load_ahead():
+            while waiting and (waiting[0][0] != "chi" or len(chi_raw) - len([u for u in grouped if u[0] == "chi"]) < 8):
+                load(waiting[0])
+                waiting.remove(waiting[0])
+
+        load_ahead()
+
+        k_banks = []
+
+        def kappa_cast():
             nc.vector.tensor_copy(out=k_rows32[:], in_=k_rows[:])
-            k_bank = psum.tile([P, 4, P], F32, name="k_bank", tag="acc", bufs=OPEN)
-            nc.tensor.transpose(k_bank[:, 0, :], k_rows32[:], identity[:])
-            nc.vector.tensor_copy(out=k_cols[:], in_=k_bank[:, 0, 0:BLOCKS])
+
+        def kappa_turn():
+            bank = psum.tile([P, 4, P], F32, name="k_bank", tag="acc%d" % (OPEN - 1 - len(k_banks)), bufs=1)
+            nc.tensor.transpose(bank[:, 0, :], k_rows32[:], identity[:])
+            k_banks.append(bank)
+
+        def kappa_square():
+            nc.vector.tensor_copy(out=k_cols[:], in_=k_banks[0][:, 0, 0:BLOCKS])
+
+        def kappa_square2():
             nc.vector.scalar_tensor_tensor(
                 out=minus_k2_cols[:], in0=k_cols[:], scalar=-1.0, in1=k_cols[:], op0=ALU.mult, op1=ALU.mult
             )
 
-        k_banks = []
-
         def kappa_spread():
             for half in range(2):
-                k_bank = psum.tile([P, 4, P], F32, name="k_bank", tag="acc", bufs=OPEN)
+                k_bank = psum.tile([P, 4, P], F32, name="k_bank", tag="acc%d" % (OPEN - 1 - len(k_banks)), bufs=1)
                 for s in range(4):
                     m = half * 4 + s
                     nc.tensor.transpose(k_bank[:, s, :], minus_k2_cols[:, m : m + 1].to_broadcast([P, P]), identity[:])
@@ -202,70 +224,61 @@ def tile_wilson_schur_hop_s2_kernel(tc, psi, chi_in, chi_halo, hop_in, hop_halo,
         def kappa_back():
             for half in range(2):
                 nc.scalar.copy(
-                    out=minus_k2[:, half * HALF : (half + 1) * HALF], in_=k_banks[half][:].rearrange("p s n -> p (s n)")
+                    out=minus_k2[:, half * HALF : (half + 1) * HALF], in_=k_banks[1 + half][:].rearrange("p s n -> p (s n)")
                 )
 
-        units = []
-        for chunk in order:
-            units += [("halo", chunk[1], 0), ("halo", chunk[1], 1)] if chunk[0] == "halo" else [chunk]
-        have_hop, have_halo, have_chi, counts = [], [], [], {}
+        ready, opened, closed, scaled, done = set(), [], [], [], {}
 
-        def newly_enabled(unit):
-            kind, i = unit[0], unit[1]
-            if kind == "hop":
-                if i >= OPEN:
-                    return []
-                have_hop.append(i)
-                return [(i, p) for p in have_chi if p < INNER or (p - INNER, i // 4) in have_halo]
-            if kind == "chi":
-                have_chi.append(i)
-                return [(b, i) for b in have_hop if i < INNER or (i - INNER, b // 4) in have_halo]
-            have_halo.append((i, unit[2]))
-            return [(b, INNER + i) for b in have_hop if INNER + i in have_chi and b // 4 == unit[2]]
+        def stationary_of(b, p):
+            return ("hop", b) if p < INNER else ("halo", p - INNER, b // 4)
+
+        def multiply_ready():
+            for n in range(2):
+                for b in range(BLOCKS):
+                    if done.get((b, n), 0) == PASSES:
+                        continue
+                    passes = [p for p in range(PASSES) if stationary_of(b, p) in ready and ("chi", p, n) in ready]
+                    passes = [p for p in passes if (b, n, p) not in done]
+                    if n == 1 and done.get((b, n), 0) + len(passes) < PASSES:
+                        passes = [p for p in passes if p < FIRST]
+                    if not passes or ((b, n) not in opened and len(opened) == OPEN):
+                        continue
+                    if (b, n) not in opened:
+                        opened.append((b, n))
+                    for p in passes:
+                        count = done.get((b, n), 0) + 1
+                        multiply(b, n, p, count == 1, count == PASSES)
+                        done[b, n], done[b, n, p] = count, True
+                    if done[b, n] == PASSES:
+                        closed.append((b, n))
+
+        def drain(c, f):
+            now = scaled[:f]
+            for x in closed[:c]:
+                scale(*x)
+                opened.remove(x)
+                scaled.append(x)
+            for x in now:
+                finish(*x)
+                scaled.remove(x)
+            for x in [x for x in closed if x not in opened]:
+                closed.remove(x)
 
         turn(units[0][1])
-        kappa_front()
-        kappa_spread()
-        for i in range(len(units) + LAG + 1):
+        i = 0
+        while i < len(units) + LAG + 1 or opened or scaled:
             if i < len(units):
                 spread(units[i])
             if i + 1 < len(units) and units[i + 1][0] == "hop":
                 turn(units[i + 1][1])
-            if i == 6:
-                kappa_back()
+            load_ahead()
+            for s, stage_fn in enumerate((kappa_cast, kappa_turn, kappa_square, kappa_square2, kappa_spread, kappa_back)):
+                if i == KAPPA + s:
+                    stage_fn()
             if 0 <= i - LAG < len(units):
                 quantize(units[i - LAG])
-            if i - LAG - 1 >= 0:
-                for b, p in newly_enabled(units[i - LAG - 1]):
-                    counts[b] = counts.get(b, 0) + 1
-                    multiply(b, 0, p, counts[b] == 1, counts[b] == PASSES)
-
-        for b in range(OPEN, BLOCKS):
-            for p in range(PASSES):
-                multiply(b, 0, p, p == 0, p == PASSES - 1)
-
-        for p in range(2, PASSES):
-            load(("chi", p, 1))
-        load(("psi", 0, 1))
-        load(("psi", 1, 1))
-        for step in LATE.split():
-            j = int(step[1:])
-            if step.startswith("x"):
-                spread(("chi", j, 1))
-            elif step.startswith("q"):
-                quantize(("chi", j, 1))
-            elif step.startswith("c"):
-                scale(j, 0)
-            else:
-                finish(j, 0)
-
-        for p in range(2):
-            for b in range(BLOCKS):
-                multiply(b, 1, p, p == 0, False)
-        for b in range(BLOCKS):
-            for p in range(2, PASSES):
-                multiply(b, 1, p, False, p == PASSES - 1)
-            scale(b, 1)
-            if b >= 1:
-                finish(b - 1, 1)
-        finish(BLOCKS - 1, 1)
+            drain(DC if i < len(units) + LAG else 8, DF if i < len(units) + LAG else DF2)
+            if 0 <= i - LAG - 1 < len(units):
+                ready.add(units[i - LAG - 1])
+            multiply_ready()
+            i += 1

from contextlib import ExitStack

import concourse.mybir as mybir
from concourse.masks import make_identity

E, KI, KH, R = 1024, 2048, 1024, 1024
FLOPS = 2 * E * R * (KI + KH) + 3 * E * R

F32 = mybir.dt.float32
BF16 = mybir.dt.bfloat16
U32 = mybir.dt.uint32
U8 = mybir.dt.uint8
E4M3 = mybir.dt.float8_e4m3fn_x4
E5M2 = mybir.dt.float8_e5m2_x4
ALU = mybir.AluOpType

P = 128
PACK = 4
K_PASS = P * PACK
INNER = KI // K_PASS
HALO = KH // K_PASS
PASSES = INNER + HALO
BLOCKS = E // P
HALF = R // 2

V_EARLY = 320
V_LATE = 64
OPEN = 6
LAG = 2
ORDER = "h0 c0 h1 c1 h2 a0 h3 c2 c3 h4 b0 a1 c4 h5 c5 h6 b1 n0 n1 n2 p0 h7 n3 n4 p2 n5 p1 p3"
DC = 2
DF = 1
FIRST = 4
DF2 = 2
KAPPA = 1
GROUPED = 8
GPSIMD_ADDS = ((0, 1), (1, 1), (2, 1), (4, 1), (6, 1))


def tile_wilson_schur_hop_s2_kernel(tc, psi, chi_in, chi_halo, hop_in, hop_halo, kappa, out):
    nc = tc.nc

    with ExitStack() as ctx:
        const = ctx.enter_context(tc.tile_pool(name="const", bufs=1))
        raw = ctx.enter_context(tc.tile_pool(name="raw", bufs=8))
        keep = ctx.enter_context(tc.tile_pool(name="keep", bufs=1))
        stage = ctx.enter_context(tc.tile_pool(name="stage", bufs=3))
        late = ctx.enter_context(tc.tile_pool(name="late", bufs=8))
        psum = ctx.enter_context(tc.psum_pool(name="psum", bufs=1))
        ctx.enter_context(tc.manual_schedule())

        hop_raw, chi_raw, halo_raw, psi_raw = {}, {}, {}, {}
        codes, planes = {}, {}
        grouped = {}
        turned = {}
        acc = {}
        product = {}
        free_banks, bank_of = list(range(OPEN)), {}

        def load(chunk):
            kind, i = chunk[0], chunk[1]
            if kind == "hop":
                tile = raw.tile([P, KI], BF16, name="hop_raw", bufs=8, align_bytes=64)
                rows = slice(i * P, (i + 1) * P)
                if i == 0:
                    for lo in (0, KI // 2):
                        nc.sync.dma_start(out=tile[:, lo : lo + KI // 2], in_=hop_in[rows, lo : lo + KI // 2])
                else:
                    nc.sync.dma_start(out=tile[:], in_=hop_in[rows, :])
                hop_raw[i] = tile
            elif kind == "chi":
                half = chunk[2]
                tile = raw.tile([P, PACK, HALF], BF16, name="chi_raw", bufs=8, align_bytes=64)
                src = chi_in if i < INNER else chi_halo
                k0 = (i if i < INNER else i - INNER) * K_PASS
                rows = src[k0 : k0 + K_PASS, half * HALF : (half + 1) * HALF]
                nc.sync.dma_start(out=tile[:], in_=rows.rearrange("(p j) r -> p j r", j=PACK))
                chi_raw[i, half] = tile
            elif kind == "halo":
                part = chunk[2]
                tile = raw.tile([P, PACK, HALF], BF16, name="halo_raw", bufs=4, align_bytes=64)
                rows = hop_halo[i * K_PASS : (i + 1) * K_PASS, part * HALF : (part + 1) * HALF]
                nc.sync.dma_start(out=tile[:], in_=rows.rearrange("(p j) e -> p j e", j=PACK))
                halo_raw[i, part] = tile
            else:
                tile = raw.tile([P, BLOCKS // 2, HALF], BF16, name="psi_raw", bufs=4, align_bytes=64)
                half = chunk[2]
                rows = psi[i * (E // 2) : (i + 1) * (E // 2), half * HALF : (half + 1) * HALF]
                nc.sync.dma_start(out=tile[:], in_=rows.rearrange("(b p) r -> p b r", p=P))
                psi_raw[i, half] = tile

        def turn(b):
            words = hop_raw[b][:].bitcast(F32)
            for h in range(2):
                bank = psum.tile([P, 4, P], F32, name="turn_bank", tag="turn", bufs=2)
                for s in range(4):
                    g, u = 2 * h + s // 2, s % 2
                    w0 = g * (K_PASS // 2)
                    nc.tensor.transpose(bank[:, s, :], words[:, w0 + u : w0 + K_PASS // 2 : 2], identity[:])
                turned[b, h] = bank

        def interleave(engine_copy, dst, src, lo, hi):
            engine_copy(
                out=dst[:, lo:hi, :].rearrange("p (c i) t -> p c t i", i=4),
                in_=src[:, :, lo:hi].rearrange("p t (c i) -> p c t i", i=4),
            )

        def spread(unit):
            kind, i = unit[0], unit[1]
            tile = stage.tile([P, 4, P, PACK], BF16, name="grouped", bufs=GROUPED, align_bytes=64)
            if kind == "hop":
                for h in range(2):
                    dst = tile[:, 2 * h : 2 * h + 2, :, :].rearrange("p g r t -> p g (r t)").bitcast(F32)
                    nc.scalar.copy(
                        out=dst.rearrange("p g (r u) -> p g r u", u=2),
                        in_=turned[i, h][:].rearrange("p (g u) r -> p g r u", u=2),
                    )
            else:
                n = unit[2]
                cut = V_EARLY if kind == "halo" or n == 0 else V_LATE
                rows = chi_raw[i, n] if kind == "chi" else halo_raw[i, n]
                flat = tile[:].rearrange("p g r t -> p (g r) t")
                interleave(nc.scalar.copy, flat, rows, cut, HALF)
                interleave(nc.vector.tensor_copy, flat, rows, 0, cut)
            grouped[unit] = tile

        def quantize(unit):
            fmt = E5M2 if unit[0] == "chi" and unit[1] >= INNER else E4M3
            name = "_".join(str(x) for x in unit)
            code = keep.tile([P, HALF], U32, name="codes_" + name, align_bytes=64)
            plane = keep.tile([P, HALF], U8, name="plane_" + name, align_bytes=64)
            nc.vector.quantize_mx(
                out=code[:].bitcast(fmt), scales=plane[:], in_=grouped[unit][:].rearrange("p g r t -> p (g r t)")
            )
            codes[unit], planes[unit] = code, plane

        def multiply(b, half, p, start, stop):
            if p < INNER:
                w, cols = ("hop", b), slice(p * P, (p + 1) * P)
            else:
                w, cols = ("halo", p - INNER, b // 4), slice(b % 4 * P, (b % 4 + 1) * P)
            x = ("chi", p, half)
            if start:
                bank = free_banks[0]
                free_banks.remove(bank)
                bank_of[b, half] = bank
                acc[b, half] = psum.tile([P, HALF], F32, name="acc_bank", tag="acc%d" % bank, bufs=1)
            nc.tensor.matmul_mx(
                out=acc[b, half][:],
                lhsT=codes[w][:, cols].bitcast(E4M3),
                lhsT_scale=planes[w][:, cols],
                rhs=codes[x][:].bitcast(E4M3 if p < INNER else E5M2),
                rhs_scale=planes[x][:],
                start=start,
                stop=stop,
            )

        def scale(b, half):
            t = late.tile([P, HALF], F32, name="product", bufs=8)
            nc.vector.tensor_tensor(
                out=t[:], in0=acc[b, half][:], in1=minus_k2[:, half * HALF : (half + 1) * HALF], op=ALU.mult
            )
            product[b, half] = t
            free_banks.append(bank_of[b, half])

        def finish(b, half):
            o = late.tile([P, HALF], F32, name="result", bufs=6)
            engine = nc.gpsimd if (b, half) in GPSIMD_ADDS else nc.vector
            field = psi_raw[b // 4, half][:, b % 4, :]
            engine.tensor_tensor(out=o[:], in0=product[b, half][:], in1=field, op=ALU.add)
            nc.sync.dma_start(out=out[b * P : (b + 1) * P, half * HALF : (half + 1) * HALF], in_=o[:])

        def eval_chunk(x):
            i = int(x[1])
            return {"h": ("hop", i), "c": ("chi", i, 0), "n": ("chi", i, 1), "a": ("halo", i, 0), "b": ("halo", i, 1), "p": ("psi", i // 2, i % 2)}[x[0]]

        identity = const.tile([P, P], F32, name="identity")
        make_identity(nc, identity[:])
        k_rows = const.tile([P, P], BF16, name="k_rows")
        nc.vector.memset(k_rows[:], 0.0)
        nc.scalar.dma_start(out=k_rows[0:BLOCKS, :], in_=kappa.rearrange("(m j) -> m j", j=P))
        k_rows32 = const.tile([P, P], F32, name="k_rows32")
        k_cols = const.tile([P, BLOCKS], F32, name="k_cols")
        minus_k2_cols = const.tile([P, BLOCKS], F32, name="minus_k2_cols")
        minus_k2 = const.tile([P, R], F32, name="minus_k2")

        loads = [eval_chunk(x) for x in ORDER.split()]
        units = [u for u in loads if u[0] != "psi"]
        waiting = list(loads)

        def load_ahead():
            while waiting and (waiting[0][0] != "chi" or len(chi_raw) - len([u for u in grouped if u[0] == "chi"]) < 8):
                load(waiting[0])
                waiting.remove(waiting[0])

        load_ahead()

        k_banks = []

        def kappa_cast():
            nc.vector.tensor_copy(out=k_rows32[:], in_=k_rows[:])

        def kappa_turn():
            bank = psum.tile([P, 4, P], F32, name="k_bank", tag="acc%d" % (OPEN - 1 - len(k_banks)), bufs=1)
            nc.tensor.transpose(bank[:, 0, :], k_rows32[:], identity[:])
            k_banks.append(bank)

        def kappa_square():
            nc.vector.tensor_copy(out=k_cols[:], in_=k_banks[0][:, 0, 0:BLOCKS])

        def kappa_square2():
            nc.vector.scalar_tensor_tensor(
                out=minus_k2_cols[:], in0=k_cols[:], scalar=-1.0, in1=k_cols[:], op0=ALU.mult, op1=ALU.mult
            )

        def kappa_spread():
            for half in range(2):
                k_bank = psum.tile([P, 4, P], F32, name="k_bank", tag="acc%d" % (OPEN - 1 - len(k_banks)), bufs=1)
                for s in range(4):
                    m = half * 4 + s
                    nc.tensor.transpose(k_bank[:, s, :], minus_k2_cols[:, m : m + 1].to_broadcast([P, P]), identity[:])
                k_banks.append(k_bank)

        def kappa_back():
            for half in range(2):
                nc.scalar.copy(
                    out=minus_k2[:, half * HALF : (half + 1) * HALF], in_=k_banks[1 + half][:].rearrange("p s n -> p (s n)")
                )

        ready, opened, closed, scaled, done = set(), [], [], [], {}

        def stationary_of(b, p):
            return ("hop", b) if p < INNER else ("halo", p - INNER, b // 4)

        def multiply_ready():
            for n in range(2):
                for b in range(BLOCKS):
                    if done.get((b, n), 0) == PASSES:
                        continue
                    passes = [p for p in range(PASSES) if stationary_of(b, p) in ready and ("chi", p, n) in ready]
                    passes = [p for p in passes if (b, n, p) not in done]
                    if n == 1 and done.get((b, n), 0) + len(passes) < PASSES:
                        passes = [p for p in passes if p < FIRST]
                    if not passes or ((b, n) not in opened and len(opened) == OPEN):
                        continue
                    if (b, n) not in opened:
                        opened.append((b, n))
                    for p in passes:
                        count = done.get((b, n), 0) + 1
                        multiply(b, n, p, count == 1, count == PASSES)
                        done[b, n], done[b, n, p] = count, True
                    if done[b, n] == PASSES:
                        closed.append((b, n))

        def drain(c, f):
            now = scaled[:f]
            for x in closed[:c]:
                scale(*x)
                opened.remove(x)
                scaled.append(x)
            for x in now:
                finish(*x)
                scaled.remove(x)
            for x in [x for x in closed if x not in opened]:
                closed.remove(x)

        turn(units[0][1])
        i = 0
        while i < len(units) + LAG + 1 or opened or scaled:
            if i < len(units):
                spread(units[i])
            if i + 1 < len(units) and units[i + 1][0] == "hop":
                turn(units[i + 1][1])
            load_ahead()
            for s, stage_fn in enumerate((kappa_cast, kappa_turn, kappa_square, kappa_square2, kappa_spread, kappa_back)):
                if i == KAPPA + s:
                    stage_fn()
            if 0 <= i - LAG < len(units):
                quantize(units[i - LAG])
            drain(DC if i < len(units) + LAG else 8, DF if i < len(units) + LAG else DF2)
            if 0 <= i - LAG - 1 < len(units):
                ready.add(units[i - LAG - 1])
            multiply_ready()
            i += 1
